import numpy as np
import ml_dtypes


def mxq(x, axis, fmt="e4m3"):
    dtype, down = {"e4m3": (ml_dtypes.float8_e4m3fn, 7), "e5m2": (ml_dtypes.float8_e5m2, 14)}[fmt]
    v = np.moveaxis(np.asarray(x, np.float32).astype(ml_dtypes.bfloat16).astype(np.float64), axis, -1)
    blocks = v.reshape(v.shape[:-1] + (-1, 32))
    amax = np.abs(blocks).max(-1, keepdims=True)
    byte = np.maximum(np.where(amax > 0, np.frexp(amax)[1] - 1 + 127, 0) - down, 1)
    scale = np.exp2(byte - 127.0)
    codes = (blocks / scale).astype(np.float32).astype(dtype).astype(np.float64)
    return np.moveaxis((codes * scale).reshape(v.shape), -1, axis)


WIDE = False


def mx_kscale(k):
    if not WIDE:
        return np.ones(k)
    levels = np.array([10, -10, 5, -5, 0])
    if k % 512:
        return np.exp2(np.random.permutation(np.resize(levels, k // 32))).repeat(32)
    a = np.empty((k // 512, 16))
    for p in range(k // 512):
        a[p, :8] = np.random.permutation(np.resize(levels, 8))
        for g in range(8):
            far = levels[np.abs(levels - a[p, g]) >= 10]
            a[p, g + 8] = far[np.random.randint(len(far))]
    return np.exp2(a.ravel()).repeat(32)


def f64(x):
    return np.asarray(x).astype(np.float64)


def striped8(idx):
    return np.concatenate([v.reshape(-1, 16).T for v in idx]).astype(np.uint16)


def unstriped8(offs):
    return np.stack([offs[16 * g:16 * g + 16].T.reshape(-1) for g in range(8)]).astype(np.int64)


E2M1 = np.array([0.0, 0.5, 1.0, 1.5, 2.0, 3.0, 4.0, 6.0, -0.0, -0.5, -1.0, -1.5, -2.0, -3.0, -4.0, -6.0])


def pack_weight(w, fmt):
    k, n = w.shape
    w = f64(np.asarray(w, np.float32).astype(ml_dtypes.bfloat16)).reshape(k // 32, 32, n)
    amax = np.abs(w).max(1)
    if fmt == "e4m3":
        byte = np.frexp(amax)[1] - 1 + 127 - 7
    else:
        mant, ex = np.frexp(amax / 6.0)
        byte = np.where(mant > 0.5, ex, ex - 1) + 127
    byte = np.clip(np.where(amax > 0, byte, 1), 1, 254)
    scaled = (w * np.exp2(127.0 - byte)[:, None, :]).reshape(k, n).astype(np.float32)
    by_word = np.ascontiguousarray(scaled.reshape(k // 512, 128, 4, n).transpose(0, 1, 3, 2))
    if fmt == "e4m3":
        words = by_word.astype(ml_dtypes.float8_e4m3fn).view(np.uint8)
    else:
        c = by_word.astype(ml_dtypes.float4_e2m1fn).view(np.uint8) & 0xF
        words = (c[..., 0::2] | (c[..., 1::2] << 4)).reshape(k // 512, 128, 2 * n)
    return np.ascontiguousarray(words), np.ascontiguousarray(byte.astype(np.uint8).reshape(k // 512, 16, n))


def unpack_weight(words, scales, fmt):
    g, _, n = scales.shape
    words = np.ascontiguousarray(words).reshape(g, 128, n, -1)
    if fmt == "e4m3":
        vals = words.view(ml_dtypes.float8_e4m3fn).astype(np.float64)
    else:
        nib = np.empty((g, 128, n, 4), np.uint8)
        nib[..., 0::2] = words & 0xF
        nib[..., 1::2] = words >> 4
        vals = E2M1[nib]
    vals = vals * np.repeat(np.exp2(scales.astype(np.float64) - 127.0), 8, axis=1)[..., None]
    return vals.transpose(0, 1, 3, 2).reshape(g * 512, n)


G, K, M, T, S = 4, 1024, 256, 4096, 512


def setup_inputs():
    n = np.random.standard_normal
    s = mx_kscale(K)[:, None]
    p_w = pack_weight(n((K, M)) / np.sqrt(K) / s, "e4m3")
    return {
        "xT": (n((K, T)) * s).astype(np.float32),
        "w_words": p_w[0],
        "w_scales": p_w[1],
        "wgt": np.repeat(np.random.uniform(0.5, 2.0, (8, G * S)), 16, axis=0).astype(np.float32),
        "b": (0.3 * n(256)).astype(np.float32),
        "offs": striped8(np.stack([np.concatenate([np.random.permutation(T)[:S] for _ in range(G)]) for _ in range(8)])),
    }


def reference(xT, w_words, w_scales, wgt, b, offs):
    idx = unstriped8(offs)
    group = np.arange(K) % 512 // 64
    xg = f64(wgt)[np.arange(K) // 4 % 128] * f64(xT)[np.arange(K)[:, None], idx[group]]
    xT_ = mxq(xg, 0, "e4m3")
    xT_ = xT_.reshape(K, G, S).sum(1)
    w_ = unpack_weight(w_words, w_scales, "e4m3")
    y = w_.T @ xT_
    return y + f64(b)[:, None]

@@ -1,0 +1,147 @@
+from contextlib import ExitStack
+
+import concourse.mybir as mybir
+from concourse.masks import make_identity
+
+G, K, M, T, S = 4, 1024, 256, 4096, 512
+FLOPS = 2 * G * K * M * S
+
+F32 = mybir.dt.float32
+BF16 = mybir.dt.bfloat16
+I32 = mybir.dt.int32
+U32 = mybir.dt.uint32
+U16 = mybir.dt.uint16
+U8 = mybir.dt.uint8
+FP8X4 = mybir.dt.float8_e4m3fn_x4
+MULT = mybir.AluOpType.mult
+ADD = mybir.AluOpType.add
+IDENTITY = mybir.ActivationFunctionType.Identity
+
+P = 128
+PACK = 4
+PASSES = K // (P * PACK)
+LISTS = 8
+GROUP = P // LISTS
+ENTRIES = G * S
+HALF = S // 2
+
+
+def tile_list_hbag_bias_kernel(tc, xT, w_words, w_scales, wgt, b, offs, out):
+    nc = tc.nc
+    with ExitStack() as ctx:
+        keep = ctx.enter_context(tc.tile_pool(name="keep", bufs=1))
+        ring = ctx.enter_context(tc.tile_pool(name="ring", bufs=2))
+        psum = ctx.enter_context(tc.psum_pool(name="psum", bufs=1))
+
+        folded = keep.tile([P, P], F32, name="folded")
+        nc.sync.dma_start(folded[:], wgt[0:P:GROUP, :].rearrange("g (t j) -> g t j", j=P))
+
+        x_rows = xT.rearrange("(a p i) t -> a i p t", p=P, i=PACK)
+        planes = [keep.tile([P, T], F32, name=f"plane{n}") for n in range(PASSES * PACK)]
+
+        def load_plane(n):
+            nc.sync.dma_start(planes[n][:], x_rows[n // PACK, n % PACK])
+
+        load_plane(0)
+        offsets = keep.tile([P, ENTRIES // GROUP], U16, name="offsets")
+        nc.sync.dma_start(offsets[:], offs)
+        for n in range(1, 6):
+            load_plane(n)
+
+        w_codes = keep.tile([P, PASSES, M], U32, name="w_codes", align_bytes=64)
+        nc.sync.dma_start(w_codes[:].bitcast(I32), w_words.rearrange("a p n t -> p a (n t)").bitcast(I32))
+        w_plane = keep.tile([P, M], U8, name="w_plane", align_bytes=64)
+        nc.gpsimd.memset(w_plane[:].bitcast(I32), 0)
+        for q in range(4):
+            nc.sync.dma_start(
+                w_plane[32 * q : 32 * q + 4 * PASSES, :].bitcast(I32),
+                w_scales[:, 4 * q : 4 * q + 4, :].bitcast(I32),
+            )
+        for n in range(6, PASSES * PACK):
+            load_plane(n)
+        bias = keep.tile([P, M // P], F32, name="bias")
+        with nc.allow_non_contiguous_dma(reason="one bias value a partition"):
+            nc.sync.dma_start(bias[:], b.rearrange("(m p) -> p m", p=P))
+
+        ident = keep.tile([P, P], F32, name="ident")
+        make_identity(nc, ident[:])
+        turned = psum.tile([P, P], F32, name="turned")
+        nc.tensor.transpose(turned[:], folded[:], ident[:])
+        weight = keep.tile([P, ENTRIES], F32, name="weight")
+        blocks = S // P
+        for c in range(G):
+            spread = ring.tile([P, blocks, LISTS, GROUP], F32, name="spread")
+            source = turned[:].rearrange("j (g t) -> j t g", g=LISTS)[:, blocks * c : blocks * (c + 1), :]
+            nc.vector.tensor_copy(spread[:], source.unsqueeze(3).to_broadcast([P, blocks, LISTS, GROUP]))
+            back = psum.tile([P, blocks, P], F32, name="back", bufs=3)
+            for t in range(blocks):
+                nc.tensor.transpose(back[:, t, :], spread[:, t].rearrange("j g r -> j (g r)"), ident[:])
+            nc.scalar.activation(weight[:, S * c : S * (c + 1)], back[:].rearrange("p t j -> p (t j)"), IDENTITY)
+
+        acc = [[psum.tile([P, HALF], F32, name=f"acc{h}_{m}") for m in range(M // P)] for h in range(2)]
+
+        def gather(target, plane, lo, hi):
+            window = plane[:].indirect(offsets[:, lo // GROUP : hi // GROUP])
+            nc.vector.tensor_tensor(target, window, weight[:, lo:hi], MULT)
+
+        def weave(woven, u, pair):
+            nc.scalar.copy(woven[:, :, 2 * u : 2 * u + 2], pair.rearrange("p e j -> p j e"))
+
+        def multiply(codes, scales, a, c, h):
+            for m in range(M // P):
+                nc.tensor.matmul_mx(
+                    out=acc[h][m][:],
+                    lhsT=w_codes[:, a, P * m : P * (m + 1)].bitcast(FP8X4),
+                    lhsT_scale=w_plane[4 * a : P, P * m : P * (m + 1)],
+                    rhs=codes.bitcast(FP8X4),
+                    rhs_scale=scales,
+                    start=(a == 0 and c == 0),
+                    stop=(a == PASSES - 1 and c == G - 1),
+                )
+
+        def finish(h):
+            cols = slice(HALF * h, HALF * (h + 1))
+            first = keep.tile([P, HALF], F32, name=f"first{h}")
+            nc.scalar.activation(first[:], acc[h][0][:], IDENTITY, bias=bias[:, 0:1])
+            nc.scalar.dma_start(out[0:P, cols], first[:])
+            second = keep.tile([P, HALF], F32, name=f"second{h}")
+            nc.vector.tensor_scalar(second[:], acc[h][1][:], bias[:, 1:2], None, ADD)
+            nc.sync.dma_start(out[P : 2 * P, cols], second[:])
+
+        for a in range(PASSES):
+            woven = keep.tile([P, ENTRIES * PACK], BF16, name="woven", align_bytes=64)
+            words = woven[:].rearrange("p (j i) -> p j i", i=PACK)
+            low = keep.tile([P, 2, ENTRIES], F32, name="low")
+            width = S if a == 0 else ENTRIES
+            for lo in range(0, ENTRIES, width):
+                gather(low[:, 0, lo : lo + width], planes[PACK * a], lo, lo + width)
+            for lo in range(0, ENTRIES, 2 * S):
+                gather(low[:, 1, lo : lo + 2 * S], planes[PACK * a + 1], lo, lo + 2 * S)
+                weave(words[:, lo : lo + 2 * S, :], 0, low[:, :, lo : lo + 2 * S])
+
+            unit, lag = (HALF, 3) if a == PASSES - 1 else (S, G)
+            units = ENTRIES // unit
+            high = keep.tile([P, units + lag, unit], F32, name="high")
+            gather(high[:, 0:units, :].rearrange("p n j -> p (n j)"), planes[PACK * a + 2], 0, ENTRIES)
+            for n in range(units + lag):
+                if n >= lag:
+                    first = unit * (n - lag)
+                    codes = keep.tile([P, unit], U32, name=f"codes{a}_{n}", align_bytes=64)
+                    scales = keep.tile([P, unit], U8, name=f"scales{a}_{n}", align_bytes=64)
+                    nc.vector.quantize_mx(
+                        out=codes[:].bitcast(FP8X4),
+                        scales=scales[:],
+                        in_=woven[:, PACK * first : PACK * (first + unit)],
+                    )
+                    for lo in range(0, unit, HALF):
+                        c, h = divmod((first + lo) // HALF, 2)
+                        multiply(codes[:, lo : lo + HALF], scales[:, lo : lo + HALF], a, c, h)
+                        if a == PASSES - 1 and c == G - 1:
+                            finish(h)
+                if n < units:
+                    row = units + n % lag
+                    width = unit // 2 if (n == 0 and a == PASSES - 1) else unit
+                    for lo in range(0, unit, width):
+                        first = unit * n + lo
+                        gather(high[:, row, lo : lo + width], planes[PACK * a + 3], first, first + width)
+                        weave(words[:, first : first + width, :], 1, high[:, n : row + 1 : row - n, lo : lo + width])

@@ -19,25 +19,28 @@ IDENTITY = mybir.ActivationFunctionType.Identity
 
 P = 128
 PACK = 4
-PASSES = K // (P * PACK)
 LISTS = 8
 GROUP = P // LISTS
+QUADRANT = 32
+SCALE_ROWS = 4
 ENTRIES = G * S
-HALF = S // 2
+UNIT = S // 2
+UNITS = ENTRIES // UNIT
+RING = 4
+PLANES_BEFORE_W = 6
 
 
 def tile_list_hbag_bias_kernel(tc, xT, w_words, w_scales, wgt, b, offs, out):
     nc = tc.nc
     with ExitStack() as ctx:
         keep = ctx.enter_context(tc.tile_pool(name="keep", bufs=1))
-        ring = ctx.enter_context(tc.tile_pool(name="ring", bufs=2))
         psum = ctx.enter_context(tc.psum_pool(name="psum", bufs=1))
 
         folded = keep.tile([P, P], F32, name="folded")
-        nc.sync.dma_start(folded[:], wgt[0:P:GROUP, :].rearrange("g (t j) -> g t j", j=P))
+        nc.sync.dma_start(folded[:], wgt[0:P:GROUP, :].rearrange("g (t j) -> t g j", j=P))
 
         x_rows = xT.rearrange("(a p i) t -> a i p t", p=P, i=PACK)
-        planes = [keep.tile([P, T], F32, name=f"plane{n}") for n in range(PASSES * PACK)]
+        planes = [keep.tile([P, T], F32, name=f"plane{n}", align_bytes=64) for n in range(K // P)]
 
         def load_plane(n):
             nc.sync.dma_start(planes[n][:], x_rows[n // PACK, n % PACK])
@@ -45,103 +48,120 @@ def tile_list_hbag_bias_kernel(tc, xT, w_words, w_scales, wgt, b, offs, out):
         load_plane(0)
         offsets = keep.tile([P, ENTRIES // GROUP], U16, name="offsets")
         nc.sync.dma_start(offsets[:], offs)
-        for n in range(1, 6):
+        for n in range(1, PLANES_BEFORE_W):
             load_plane(n)
 
-        w_codes = keep.tile([P, PASSES, M], U32, name="w_codes", align_bytes=64)
-        nc.sync.dma_start(w_codes[:].bitcast(I32), w_words.rearrange("a p n t -> p a (n t)").bitcast(I32))
-        w_plane = keep.tile([P, M], U8, name="w_plane", align_bytes=64)
-        nc.gpsimd.memset(w_plane[:].bitcast(I32), 0)
-        for q in range(4):
+        w_codes = keep.tile([P, 2, M], U32, name="w_codes", align_bytes=64)
+        nc.sync.dma_start(w_codes[:].bitcast(I32), w_words.rearrange("a p n i -> p a (n i)").bitcast(I32))
+        w_scale = keep.tile([P, M], U8, name="w_scale", align_bytes=64)
+        nc.gpsimd.memset(w_scale[:].bitcast(I32), 0)
+        for q in range(P // QUADRANT):
             nc.sync.dma_start(
-                w_plane[32 * q : 32 * q + 4 * PASSES, :].bitcast(I32),
-                w_scales[:, 4 * q : 4 * q + 4, :].bitcast(I32),
+                w_scale[QUADRANT * q : QUADRANT * q + 2 * SCALE_ROWS, :].bitcast(I32),
+                w_scales[:, SCALE_ROWS * q : SCALE_ROWS * (q + 1), :].bitcast(I32),
             )
-        for n in range(6, PASSES * PACK):
+        for n in range(PLANES_BEFORE_W, K // P):
             load_plane(n)
         bias = keep.tile([P, M // P], F32, name="bias")
-        with nc.allow_non_contiguous_dma(reason="one bias value a partition"):
-            nc.sync.dma_start(bias[:], b.rearrange("(m p) -> p m", p=P))
+        with nc.allow_non_contiguous_dma(reason="one bias value for each partition and half of out's rows"):
+            nc.sync.dma_start(bias[:], b.rearrange("(r p) -> p r", p=P))
 
         ident = keep.tile([P, P], F32, name="ident")
         make_identity(nc, ident[:])
-        turned = psum.tile([P, P], F32, name="turned")
-        nc.tensor.transpose(turned[:], folded[:], ident[:])
-        weight = keep.tile([P, ENTRIES], F32, name="weight")
+        turned_bank = psum.tile([P, P], F32, name="turned_bank")
+        nc.tensor.transpose(turned_bank[:], folded[:], ident[:])
+        turned = keep.tile([P, P], F32, name="turned")
+        nc.vector.tensor_copy(turned[:], turned_bank[:])
         blocks = S // P
+        spread = keep.tile([P, G, blocks, LISTS, GROUP], F32, name="spread")
+        weight = keep.tile([P, ENTRIES], F32, name="weight")
         for c in range(G):
-            spread = ring.tile([P, blocks, LISTS, GROUP], F32, name="spread")
-            source = turned[:].rearrange("j (g t) -> j t g", g=LISTS)[:, blocks * c : blocks * (c + 1), :]
-            nc.vector.tensor_copy(spread[:], source.unsqueeze(3).to_broadcast([P, blocks, LISTS, GROUP]))
+            source = turned[:].rearrange("j (t g) -> j t g", g=LISTS)[:, blocks * c : blocks * (c + 1), :]
+            nc.vector.tensor_copy(spread[:, c], source.unsqueeze(3).to_broadcast([P, blocks, LISTS, GROUP]))
             back = psum.tile([P, blocks, P], F32, name="back", bufs=3)
             for t in range(blocks):
-                nc.tensor.transpose(back[:, t, :], spread[:, t].rearrange("j g r -> j (g r)"), ident[:])
+                nc.tensor.transpose(back[:, t, :], spread[:, c, t].rearrange("j g r -> j (g r)"), ident[:])
             nc.scalar.activation(weight[:, S * c : S * (c + 1)], back[:].rearrange("p t j -> p (t j)"), IDENTITY)
 
-        acc = [[psum.tile([P, HALF], F32, name=f"acc{h}_{m}") for m in range(M // P)] for h in range(2)]
+        sums = [[psum.tile([P, UNIT], F32, name=f"sum{h}_{r}") for r in range(M // P)] for h in range(2)]
 
-        def gather(target, plane, lo, hi):
-            window = plane[:].indirect(offsets[:, lo // GROUP : hi // GROUP])
+        def gather(target, n, lo, hi):
+            window = planes[n][:].indirect(offsets[:, lo // GROUP : hi // GROUP])
             nc.vector.tensor_tensor(target, window, weight[:, lo:hi], MULT)
 
-        def weave(woven, u, pair):
-            nc.scalar.copy(woven[:, :, 2 * u : 2 * u + 2], pair.rearrange("p e j -> p j e"))
+        def weave(woven, lo, hi, i, pair):
+            words = woven[:, PACK * lo : PACK * hi].rearrange("p (m i) -> p m i", i=PACK)
+            nc.scalar.copy(words[:, :, i : i + 2], pair.rearrange("p i m -> p m i"))
 
-        def multiply(codes, scales, a, c, h):
-            for m in range(M // P):
+        def quantise(codes, scales, woven, lo, hi):
+            nc.vector.quantize_mx(out=codes.bitcast(FP8X4), scales=scales, in_=woven[:, PACK * lo : PACK * hi])
+
+        def multiply(codes, scales, a, u):
+            c, h = divmod(u, 2)
+            for r in range(M // P):
                 nc.tensor.matmul_mx(
-                    out=acc[h][m][:],
-                    lhsT=w_codes[:, a, P * m : P * (m + 1)].bitcast(FP8X4),
-                    lhsT_scale=w_plane[4 * a : P, P * m : P * (m + 1)],
+                    out=sums[h][r][:],
+                    lhsT=w_codes[:, a, P * r : P * (r + 1)].bitcast(FP8X4),
+                    lhsT_scale=w_scale[SCALE_ROWS * a : P, P * r : P * (r + 1)],
                     rhs=codes.bitcast(FP8X4),
                     rhs_scale=scales,
                     start=(a == 0 and c == 0),
-                    stop=(a == PASSES - 1 and c == G - 1),
+                    stop=(a == 1 and c == G - 1),
                 )
 
-        def finish(h):
-            cols = slice(HALF * h, HALF * (h + 1))
-            first = keep.tile([P, HALF], F32, name=f"first{h}")
-            nc.scalar.activation(first[:], acc[h][0][:], IDENTITY, bias=bias[:, 0:1])
-            nc.scalar.dma_start(out[0:P, cols], first[:])
-            second = keep.tile([P, HALF], F32, name=f"second{h}")
-            nc.vector.tensor_scalar(second[:], acc[h][1][:], bias[:, 1:2], None, ADD)
-            nc.sync.dma_start(out[P : 2 * P, cols], second[:])
+        def store(h):
+            cols = slice(UNIT * h, UNIT * (h + 1))
+            upper = keep.tile([P, UNIT], F32, name=f"upper{h}")
+            nc.scalar.activation(upper[:], sums[h][0][:], IDENTITY, bias=bias[:, 0:1])
+            nc.scalar.dma_start(out[0:P, cols], upper[:])
+            lower = keep.tile([P, UNIT], F32, name=f"lower{h}")
+            nc.vector.tensor_scalar(lower[:], sums[h][1][:], bias[:, 1:2], None, ADD)
+            nc.sync.dma_start(out[P : 2 * P, cols], lower[:])
 
-        for a in range(PASSES):
-            woven = keep.tile([P, ENTRIES * PACK], BF16, name="woven", align_bytes=64)
-            words = woven[:].rearrange("p (j i) -> p j i", i=PACK)
-            low = keep.tile([P, 2, ENTRIES], F32, name="low")
-            width = S if a == 0 else ENTRIES
-            for lo in range(0, ENTRIES, width):
-                gather(low[:, 0, lo : lo + width], planes[PACK * a], lo, lo + width)
-            for lo in range(0, ENTRIES, 2 * S):
-                gather(low[:, 1, lo : lo + 2 * S], planes[PACK * a + 1], lo, lo + 2 * S)
-                weave(words[:, lo : lo + 2 * S, :], 0, low[:, :, lo : lo + 2 * S])
+        def gather_and_weave(pair, n, woven):
+            for lo in range(0, ENTRIES, ENTRIES // 2):
+                hi = lo + ENTRIES // 2
+                gather(pair[:, 1, lo:hi], n, lo, hi)
+                weave(woven, lo, hi, n % PACK - 1, pair[:, :, lo:hi])
 
-            unit, lag = (HALF, 3) if a == PASSES - 1 else (S, G)
-            units = ENTRIES // unit
-            high = keep.tile([P, units + lag, unit], F32, name="high")
-            gather(high[:, 0:units, :].rearrange("p n j -> p (n j)"), planes[PACK * a + 2], 0, ENTRIES)
-            for n in range(units + lag):
-                if n >= lag:
-                    first = unit * (n - lag)
-                    codes = keep.tile([P, unit], U32, name=f"codes{a}_{n}", align_bytes=64)
-                    scales = keep.tile([P, unit], U8, name=f"scales{a}_{n}", align_bytes=64)
-                    nc.vector.quantize_mx(
-                        out=codes[:].bitcast(FP8X4),
-                        scales=scales[:],
-                        in_=woven[:, PACK * first : PACK * (first + unit)],
-                    )
-                    for lo in range(0, unit, HALF):
-                        c, h = divmod((first + lo) // HALF, 2)
-                        multiply(codes[:, lo : lo + HALF], scales[:, lo : lo + HALF], a, c, h)
-                        if a == PASSES - 1 and c == G - 1:
-                            finish(h)
-                if n < units:
-                    row = units + n % lag
-                    width = unit // 2 if (n == 0 and a == PASSES - 1) else unit
-                    for lo in range(0, unit, width):
-                        first = unit * n + lo
-                        gather(high[:, row, lo : lo + width], planes[PACK * a + 3], first, first + width)
-                        weave(words[:, first : first + width, :], 1, high[:, n : row + 1 : row - n, lo : lo + width])
+        woven0 = keep.tile([P, ENTRIES * PACK], BF16, name="woven0", align_bytes=64)
+        pair = keep.tile([P, 2, ENTRIES], F32, name="pair_low")
+        for lo, hi in ((0, S), (S, 2 * S), (2 * S, ENTRIES)):
+            gather(pair[:, 0, lo:hi], 0, lo, hi)
+        gather_and_weave(pair, 1, woven0)
+        pair = keep.tile([P, 2, ENTRIES], F32, name="pair_high")
+        gather(pair[:, 0], 2, 0, ENTRIES)
+        gather_and_weave(pair, 3, woven0)
+
+        pair = keep.tile([P, 2, ENTRIES], F32, name="pair_low")
+        gather(pair[:, 0], PACK, 0, ENTRIES)
+        codes0 = keep.tile([P, ENTRIES], U32, name=f"plane{PACK}", align_bytes=64)
+        scales0 = keep.tile([P, ENTRIES], U8, name="scales0", align_bytes=64)
+        for lo in range(0, ENTRIES, ENTRIES // 2):
+            hi = lo + ENTRIES // 2
+            quantise(codes0[:, lo:hi], scales0[:, lo:hi], woven0, lo, hi)
+        for u in range(UNITS):
+            multiply(codes0[:, UNIT * u : UNIT * (u + 1)], scales0[:, UNIT * u : UNIT * (u + 1)], 0, u)
+
+        woven1 = keep.tile([P, ENTRIES * PACK], BF16, name="woven1", align_bytes=64)
+        gather_and_weave(pair, PACK + 1, woven1)
+
+        rows = keep.tile([P, UNITS + RING, UNIT], F32, name="pair_high")
+        gather(rows[:, 0:UNITS, :].rearrange("p u j -> p (u j)"), PACK + 2, 0, ENTRIES)
+        for step in range(UNITS + RING):
+            if step >= RING:
+                u = step - RING
+                codes1 = keep.tile([P, UNIT], U32, name=f"codes1_{u}", align_bytes=64)
+                scales1 = keep.tile([P, UNIT], U8, name=f"scales1_{u}", align_bytes=64)
+                quantise(codes1[:], scales1[:], woven1, UNIT * u, UNIT * (u + 1))
+                multiply(codes1[:], scales1[:], 1, u)
+                if u // 2 == G - 1:
+                    store(u % 2)
+            if step < UNITS:
+                u = step
+                row = UNITS + u % RING
+                width = UNIT // 2 if u == 0 else UNIT
+                for j in range(0, UNIT, width):
+                    lo = UNIT * u + j
+                    gather(rows[:, row, j : j + width], PACK + 3, lo, lo + width)
+                    weave(woven1, lo, lo + width, 2, rows[:, u : row + 1 : row - u, j : j + width])

from contextlib import ExitStack

import concourse.mybir as mybir
from concourse.masks import make_identity

G, K, M, T, S = 4, 1024, 256, 4096, 512
FLOPS = 2 * G * K * M * S

F32 = mybir.dt.float32
BF16 = mybir.dt.bfloat16
I32 = mybir.dt.int32
U32 = mybir.dt.uint32
U16 = mybir.dt.uint16
U8 = mybir.dt.uint8
FP8X4 = mybir.dt.float8_e4m3fn_x4
MULT = mybir.AluOpType.mult
ADD = mybir.AluOpType.add
IDENTITY = mybir.ActivationFunctionType.Identity

P = 128
PACK = 4
LISTS = 8
GROUP = P // LISTS
QUADRANT = 32
SCALE_ROWS = 4
ENTRIES = G * S
UNIT = S // 2
UNITS = ENTRIES // UNIT
RING = 4
PLANES_BEFORE_W = 6


def tile_list_hbag_bias_kernel(tc, xT, w_words, w_scales, wgt, b, offs, out):
    nc = tc.nc
    with ExitStack() as ctx:
        keep = ctx.enter_context(tc.tile_pool(name="keep", bufs=1))
        psum = ctx.enter_context(tc.psum_pool(name="psum", bufs=1))

        folded = keep.tile([P, P], F32, name="folded")
        nc.sync.dma_start(folded[:], wgt[0:P:GROUP, :].rearrange("g (t j) -> t g j", j=P))

        x_rows = xT.rearrange("(a p i) t -> a i p t", p=P, i=PACK)
        planes = [keep.tile([P, T], F32, name=f"plane{n}", align_bytes=64) for n in range(K // P)]

        def load_plane(n):
            nc.sync.dma_start(planes[n][:], x_rows[n // PACK, n % PACK])

        load_plane(0)
        offsets = keep.tile([P, ENTRIES // GROUP], U16, name="offsets")
        nc.sync.dma_start(offsets[:], offs)
        for n in range(1, PLANES_BEFORE_W):
            load_plane(n)

        w_codes = keep.tile([P, 2, M], U32, name="w_codes", align_bytes=64)
        nc.sync.dma_start(w_codes[:].bitcast(I32), w_words.rearrange("a p n i -> p a (n i)").bitcast(I32))
        w_scale = keep.tile([P, M], U8, name="w_scale", align_bytes=64)
        nc.gpsimd.memset(w_scale[:].bitcast(I32), 0)
        for q in range(P // QUADRANT):
            nc.sync.dma_start(
                w_scale[QUADRANT * q : QUADRANT * q + 2 * SCALE_ROWS, :].bitcast(I32),
                w_scales[:, SCALE_ROWS * q : SCALE_ROWS * (q + 1), :].bitcast(I32),
            )
        for n in range(PLANES_BEFORE_W, K // P):
            load_plane(n)
        bias = keep.tile([P, M // P], F32, name="bias")
        with nc.allow_non_contiguous_dma(reason="one bias value for each partition and half of out's rows"):
            nc.sync.dma_start(bias[:], b.rearrange("(r p) -> p r", p=P))

        ident = keep.tile([P, P], F32, name="ident")
        make_identity(nc, ident[:])
        turned_bank = psum.tile([P, P], F32, name="turned_bank")
        nc.tensor.transpose(turned_bank[:], folded[:], ident[:])
        turned = keep.tile([P, P], F32, name="turned")
        nc.vector.tensor_copy(turned[:], turned_bank[:])
        blocks = S // P
        spread = keep.tile([P, G, blocks, LISTS, GROUP], F32, name="spread")
        weight = keep.tile([P, ENTRIES], F32, name="weight")
        for c in range(G):
            source = turned[:].rearrange("j (t g) -> j t g", g=LISTS)[:, blocks * c : blocks * (c + 1), :]
            nc.vector.tensor_copy(spread[:, c], source.unsqueeze(3).to_broadcast([P, blocks, LISTS, GROUP]))
            back = psum.tile([P, blocks, P], F32, name="back", bufs=3)
            for t in range(blocks):
                nc.tensor.transpose(back[:, t, :], spread[:, c, t].rearrange("j g r -> j (g r)"), ident[:])
            nc.scalar.activation(weight[:, S * c : S * (c + 1)], back[:].rearrange("p t j -> p (t j)"), IDENTITY)

        sums = [[psum.tile([P, UNIT], F32, name=f"sum{h}_{r}") for r in range(M // P)] for h in range(2)]

        def gather(target, n, lo, hi):
            window = planes[n][:].indirect(offsets[:, lo // GROUP : hi // GROUP])
            nc.vector.tensor_tensor(target, window, weight[:, lo:hi], MULT)

        def weave(woven, lo, hi, i, pair):
            words = woven[:, PACK * lo : PACK * hi].rearrange("p (m i) -> p m i", i=PACK)
            nc.scalar.copy(words[:, :, i : i + 2], pair.rearrange("p i m -> p m i"))

        def quantise(codes, scales, woven, lo, hi):
            nc.vector.quantize_mx(out=codes.bitcast(FP8X4), scales=scales, in_=woven[:, PACK * lo : PACK * hi])

        def multiply(codes, scales, a, u):
            c, h = divmod(u, 2)
            for r in range(M // P):
                nc.tensor.matmul_mx(
                    out=sums[h][r][:],
                    lhsT=w_codes[:, a, P * r : P * (r + 1)].bitcast(FP8X4),
                    lhsT_scale=w_scale[SCALE_ROWS * a : P, P * r : P * (r + 1)],
                    rhs=codes.bitcast(FP8X4),
                    rhs_scale=scales,
                    start=(a == 0 and c == 0),
                    stop=(a == 1 and c == G - 1),
                )

        def store(h):
            cols = slice(UNIT * h, UNIT * (h + 1))
            upper = keep.tile([P, UNIT], F32, name=f"upper{h}")
            nc.scalar.activation(upper[:], sums[h][0][:], IDENTITY, bias=bias[:, 0:1])
            nc.scalar.dma_start(out[0:P, cols], upper[:])
            lower = keep.tile([P, UNIT], F32, name=f"lower{h}")
            nc.vector.tensor_scalar(lower[:], sums[h][1][:], bias[:, 1:2], None, ADD)
            nc.sync.dma_start(out[P : 2 * P, cols], lower[:])

        def gather_and_weave(pair, n, woven):
            for lo in range(0, ENTRIES, ENTRIES // 2):
                hi = lo + ENTRIES // 2
                gather(pair[:, 1, lo:hi], n, lo, hi)
                weave(woven, lo, hi, n % PACK - 1, pair[:, :, lo:hi])

        woven0 = keep.tile([P, ENTRIES * PACK], BF16, name="woven0", align_bytes=64)
        pair = keep.tile([P, 2, ENTRIES], F32, name="pair_low")
        for lo, hi in ((0, S), (S, 2 * S), (2 * S, ENTRIES)):
            gather(pair[:, 0, lo:hi], 0, lo, hi)
        gather_and_weave(pair, 1, woven0)
        pair = keep.tile([P, 2, ENTRIES], F32, name="pair_high")
        gather(pair[:, 0], 2, 0, ENTRIES)
        gather_and_weave(pair, 3, woven0)

        pair = keep.tile([P, 2, ENTRIES], F32, name="pair_low")
        gather(pair[:, 0], PACK, 0, ENTRIES)
        codes0 = keep.tile([P, ENTRIES], U32, name=f"plane{PACK}", align_bytes=64)
        scales0 = keep.tile([P, ENTRIES], U8, name="scales0", align_bytes=64)
        for lo in range(0, ENTRIES, ENTRIES // 2):
            hi = lo + ENTRIES // 2
            quantise(codes0[:, lo:hi], scales0[:, lo:hi], woven0, lo, hi)
        for u in range(UNITS):
            multiply(codes0[:, UNIT * u : UNIT * (u + 1)], scales0[:, UNIT * u : UNIT * (u + 1)], 0, u)

        woven1 = keep.tile([P, ENTRIES * PACK], BF16, name="woven1", align_bytes=64)
        gather_and_weave(pair, PACK + 1, woven1)

        rows = keep.tile([P, UNITS + RING, UNIT], F32, name="pair_high")
        gather(rows[:, 0:UNITS, :].rearrange("p u j -> p (u j)"), PACK + 2, 0, ENTRIES)
        for step in range(UNITS + RING):
            if step >= RING:
                u = step - RING
                codes1 = keep.tile([P, UNIT], U32, name=f"codes1_{u}", align_bytes=64)
                scales1 = keep.tile([P, UNIT], U8, name=f"scales1_{u}", align_bytes=64)
                quantise(codes1[:], scales1[:], woven1, UNIT * u, UNIT * (u + 1))
                multiply(codes1[:], scales1[:], 1, u)
                if u // 2 == G - 1:
                    store(u % 2)
            if step < UNITS:
                u = step
                row = UNITS + u % RING
                width = UNIT // 2 if u == 0 else UNIT
                for j in range(0, UNIT, width):
                    lo = UNIT * u + j
                    gather(rows[:, row, j : j + width], PACK + 3, lo, lo + width)
                    weave(woven1, lo, lo + width, 2, rows[:, u : row + 1 : row - u, j : j + width])
